import numpy as np
import ml_dtypes


def mxq(x, axis, fmt="e4m3"):
    dtype, down = {"e4m3": (ml_dtypes.float8_e4m3fn, 7), "e5m2": (ml_dtypes.float8_e5m2, 14)}[fmt]
    v = np.moveaxis(np.asarray(x, np.float32).astype(ml_dtypes.bfloat16).astype(np.float64), axis, -1)
    blocks = v.reshape(v.shape[:-1] + (-1, 32))
    amax = np.abs(blocks).max(-1, keepdims=True)
    byte = np.maximum(np.where(amax > 0, np.frexp(amax)[1] - 1 + 127, 0) - down, 1)
    scale = np.exp2(byte - 127.0)
    codes = (blocks / scale).astype(np.float32).astype(dtype).astype(np.float64)
    return np.moveaxis((codes * scale).reshape(v.shape), -1, axis)


WIDE = False


def mx_kscale(k):
    if not WIDE:
        return np.ones(k)
    levels = np.array([10, -10, 5, -5, 0])
    if k % 512:
        return np.exp2(np.random.permutation(np.resize(levels, k // 32))).repeat(32)
    a = np.empty((k // 512, 16))
    for p in range(k // 512):
        a[p, :8] = np.random.permutation(np.resize(levels, 8))
        for g in range(8):
            far = levels[np.abs(levels - a[p, g]) >= 10]
            a[p, g + 8] = far[np.random.randint(len(far))]
    return np.exp2(a.ravel()).repeat(32)


def f64(x):
    return np.asarray(x).astype(np.float64)


def striped(idx):
    return np.tile(idx.reshape(-1, 16).T, (8, 1)).astype(np.uint16)


def unstriped(offs):
    return offs[:16].T.reshape(-1).astype(np.int64)


E2M1 = np.array([0.0, 0.5, 1.0, 1.5, 2.0, 3.0, 4.0, 6.0, -0.0, -0.5, -1.0, -1.5, -2.0, -3.0, -4.0, -6.0])


def pack_weight(w, fmt):
    k, n = w.shape
    w = f64(np.asarray(w, np.float32).astype(ml_dtypes.bfloat16)).reshape(k // 32, 32, n)
    amax = np.abs(w).max(1)
    if fmt == "e4m3":
        byte = np.frexp(amax)[1] - 1 + 127 - 7
    else:
        mant, ex = np.frexp(amax / 6.0)
        byte = np.where(mant > 0.5, ex, ex - 1) + 127
    byte = np.clip(np.where(amax > 0, byte, 1), 1, 254)
    scaled = (w * np.exp2(127.0 - byte)[:, None, :]).reshape(k, n).astype(np.float32)
    by_word = np.ascontiguousarray(scaled.reshape(k // 512, 128, 4, n).transpose(0, 1, 3, 2))
    if fmt == "e4m3":
        words = by_word.astype(ml_dtypes.float8_e4m3fn).view(np.uint8)
    else:
        c = by_word.astype(ml_dtypes.float4_e2m1fn).view(np.uint8) & 0xF
        words = (c[..., 0::2] | (c[..., 1::2] << 4)).reshape(k // 512, 128, 2 * n)
    return np.ascontiguousarray(words), np.ascontiguousarray(byte.astype(np.uint8).reshape(k // 512, 16, n))


def unpack_weight(words, scales, fmt):
    g, _, n = scales.shape
    words = np.ascontiguousarray(words).reshape(g, 128, n, -1)
    if fmt == "e4m3":
        vals = words.view(ml_dtypes.float8_e4m3fn).astype(np.float64)
    else:
        nib = np.empty((g, 128, n, 4), np.uint8)
        nib[..., 0::2] = words & 0xF
        nib[..., 1::2] = words >> 4
        vals = E2M1[nib]
    vals = vals * np.repeat(np.exp2(scales.astype(np.float64) - 127.0), 8, axis=1)[..., None]
    return vals.transpose(0, 1, 3, 2).reshape(g * 512, n)


def relu2(v):
    return np.maximum(v, 0.0) ** 2


K, T, E, C, H, N = 1024, 512, 8, 128, 512, 256


def by_expert(wq, xq):
    return np.concatenate([wq[e].T @ xq[:, e * C:(e + 1) * C] for e in range(E)], axis=1)


def setup_inputs():
    n = np.random.standard_normal
    s = mx_kscale(K)[:, None]
    u = mx_kscale(H)
    first = np.random.permutation(np.repeat(np.arange(E), T // E))
    second = (first + 1 + np.random.permutation(np.repeat(np.arange(E - 1), -(-T // (E - 1)))[:T])) % E
    while np.bincount(second, minlength=E).max() != T // E:
        load = np.bincount(second, minlength=E); hi, lo = int(load.argmax()), int(load.argmin())
        t = np.flatnonzero((second == hi) & (first != lo))[0]; second[t] = lo
    slot_token = np.empty(E * C, np.int64); pos = np.empty((2, T), np.int64); fill = np.zeros(E, np.int64)
    place = np.stack([np.random.permutation(C) for _ in range(E)])
    for r, deal in enumerate((first, second)):
        for t in np.random.permutation(T):
            e = deal[t]; j = e * C + place[e, fill[e]]; fill[e] += 1; slot_token[j] = t; pos[r, t] = j
    g = np.random.uniform(0.2, 0.8, T)
    w1 = [pack_weight(m, "e2m1") for m in n((E, K, H)) / np.sqrt(K) / s[None] * u[None, None, :]]
    w2 = [pack_weight(m, "e2m1") for m in n((E, H, N)) / np.sqrt(H) / u[None, :, None] ** 2]
    return {
        "xT": (n((K, T)) * s).astype(np.float32),
        "w1_words": np.stack([m[0] for m in w1]),
        "w1_scales": np.stack([m[1] for m in w1]),
        "w2_words": np.stack([m[0] for m in w2]),
        "w2_scales": np.stack([m[1] for m in w2]),
        "gate": np.stack([np.tile(g, (N, 1)), np.tile(1.0 - g, (N, 1))]).astype(np.float32),
        "offs": striped(slot_token),
        "pos1": striped(pos[0]),
        "pos2": striped(pos[1]),
    }


def reference(xT, w1_words, w1_scales, w2_words, w2_scales, gate, offs, pos1, pos2):
    idx = unstriped(offs)
    w1 = np.stack([unpack_weight(w1_words[e], w1_scales[e], "e2m1") for e in range(E)])
    w2 = np.stack([unpack_weight(w2_words[e], w2_scales[e], "e2m1") for e in range(E)])
    xq = mxq(f64(xT)[:, idx], 0, "e4m3")
    h = relu2(by_expert(w1, xq))
    y = by_expert(w2, mxq(h, 0, "e4m3"))
    return f64(gate[0]) * y[:, unstriped(pos1)] + f64(gate[1]) * y[:, unstriped(pos2)]

@@ -1,0 +1,231 @@
+from contextlib import ExitStack
+
+import concourse.mybir as mybir
+from concourse.masks import make_identity
+
+K, T, E, C, H, N = 1024, 512, 8, 128, 512, 256
+S = E * C
+P = 128
+PASSES = K // 512
+FLOPS = 2 * S * (K * H + H * N)
+
+F32 = mybir.dt.float32
+BF16 = mybir.dt.bfloat16
+I32 = mybir.dt.int32
+U32 = mybir.dt.uint32
+U16 = mybir.dt.uint16
+U8 = mybir.dt.uint8
+E4M3X4 = mybir.dt.float8_e4m3fn_x4
+E2M1X4 = mybir.dt.float4_e2m1fn_x4
+MULT = mybir.AluOpType.mult
+ADD = mybir.AluOpType.add
+MAX = mybir.AluOpType.max
+RELU = mybir.ActivationFunctionType.Relu
+SQUARE = mybir.ActivationFunctionType.Square
+
+XT = T // 2
+X_SPLIT = {(0, 0): 160, (0, 1): 160, (1, 0): 0, (1, 1): 64}
+RELU_ON_VECTOR = (6,)
+Y_ON_VECTOR = ((0, 0), (0, 1), (1, 0), (1, 1), (2, 0), (3, 0))
+
+
+def tile_moe_pln_mlp_relu2_kernel(
+    tc, xT, w1_words, w1_scales, w2_words, w2_scales, gate, offs, pos1, pos2, out
+):
+    nc = tc.nc
+    with ExitStack() as ctx:
+        lists = ctx.enter_context(tc.tile_pool(name="lists", bufs=1))
+        keep = ctx.enter_context(tc.tile_pool(name="keep", bufs=1))
+        ring = ctx.enter_context(tc.tile_pool(name="ring", bufs=3))
+        psum_a = ctx.enter_context(tc.psum_pool(name="psum_a", bufs=3))
+        psum_t = ctx.enter_context(tc.psum_pool(name="psum_t", bufs=3))
+        psum_y = ctx.enter_context(tc.psum_pool(name="psum_y", bufs=1))
+
+        offs_t = lists.tile([P, S // 16], U16, name="offs_t")
+        pos1_t = lists.tile([P, T // 16], U16, name="pos1_t")
+        pos2_t = lists.tile([P, T // 16], U16, name="pos2_t")
+
+        x_raw = {}
+        w1_pl = keep.tile([P, E * PASSES * H], U8, name="w1_pl", align_bytes=64)
+        w2_pl = keep.tile([P, E * N], U8, name="w2_pl", align_bytes=64)
+        for s in range(PASSES):
+            x_in = xT[512 * s : 512 * s + 512, :].rearrange("(p j) t -> p j t", j=4)
+            for part in range(2):
+                x_part = keep.tile([P, 4, XT], F32, name=f"x_raw{s}{part}")
+                nc.sync.dma_start(out=x_part[:], in_=x_in[:, :, XT * part : XT * part + XT])
+                x_raw[s, part] = x_part
+            if s == 0:
+                nc.sync.dma_start(offs_t[:], offs)
+
+        nc.vector.memset(w1_pl[:].bitcast(I32), 0)
+        nc.vector.memset(w2_pl[:].bitcast(I32), 0)
+        w1_pl_words = w1_pl[:].bitcast(I32).rearrange("p (g i) -> p g i", g=E * PASSES)
+        w2_pl_words = w2_pl[:].bitcast(I32).rearrange("p (g i) -> p g i", g=E)
+        w1_sc_words = w1_scales.bitcast(I32).rearrange("e s q i -> q (e s) i")
+        w2_sc_words = w2_scales.bitcast(I32).rearrange("e s q i -> q (e s) i")
+        for q in range(4):
+            nc.sync.dma_start(out=w1_pl_words[32 * q : 32 * q + 4], in_=w1_sc_words[4 * q : 4 * q + 4])
+
+        w1_in = w1_words.bitcast(I32).rearrange("e s p c -> p (e s) c")
+        w1_t = []
+        for pair in range(E // 2):
+            w1_two = keep.tile([P, 4 * 2 * H], U8, name=f"w1_two{pair}", align_bytes=64)
+            nc.sync.dma_start(
+                out=w1_two[:].bitcast(I32).rearrange("p (g c) -> p g c", g=4),
+                in_=w1_in[:, 4 * pair : 4 * pair + 4, :],
+            )
+            w1_t.append(w1_two)
+            if pair == 0:
+                for q in range(4):
+                    nc.sync.dma_start(out=w2_pl_words[32 * q : 32 * q + 4], in_=w2_sc_words[4 * q : 4 * q + 4])
+                w2_t = keep.tile([P, E * 2 * N], U8, name="w2_t", align_bytes=64)
+                nc.sync.dma_start(
+                    out=w2_t[:].bitcast(I32).rearrange("p (g c) -> p g c", g=E),
+                    in_=w2_words.bitcast(I32).rearrange("e s p c -> p (e s) c"),
+                )
+        nc.sync.dma_start(pos1_t[:], pos1)
+        nc.sync.dma_start(pos2_t[:], pos2)
+        gates = []
+        for h in range(2):
+            gate_h = keep.tile([P, 2, T], F32, name=f"gate_h{h}")
+            nc.sync.dma_start(out=gate_h[:], in_=gate[:, P * h : P * h + P, :].rearrange("g n t -> n g t"))
+            gates.append(gate_h)
+
+        warm = keep.tile([P, 1], F32, name="warm")
+        nc.gpsimd.memset(warm[:], 0.0)
+        nc.scalar.activation(warm[:], warm[:], SQUARE)
+        x_scales = [keep.tile([P, T], U8, name=f"x_scales{s}", align_bytes=64) for s in range(PASSES)]
+        for s in range(PASSES):
+            nc.gpsimd.memset(x_scales[s][:], 0)
+        ident = keep.tile([P, P], F32, name="ident")
+        make_identity(nc, ident[:])
+
+        x_codes = [keep.tile([P, T], U32, name=f"x_codes{s}", align_bytes=64) for s in range(PASSES)]
+        g_codes = [keep.tile([P, S], U32, name=f"g_codes{s}", align_bytes=64) for s in range(PASSES)]
+        g_scales = [keep.tile([P, S], U8, name=f"g_scales{s}", align_bytes=64) for s in range(PASSES)]
+
+        def tokens(s):
+            xb = keep.tile([P, T, 4], BF16, name=f"xb{s}", align_bytes=64)
+            for part in range(2):
+                a, m = XT * part, X_SPLIT[s, part]
+                view = x_raw[s, part][:].rearrange("p j t -> p t j")
+                if m > 0:
+                    nc.vector.tensor_copy(xb[:, a : a + m, :], view[:, 0:m, :])
+                if m < XT:
+                    nc.scalar.copy(xb[:, a + m : a + XT, :], view[:, m:XT, :])
+                nc.vector.quantize_mx(
+                    out=x_codes[s][:, a : a + XT].bitcast(E4M3X4),
+                    scales=x_scales[s][:, a : a + XT],
+                    in_=xb[:, a : a + XT, :].rearrange("p t j -> p (t j)"),
+                )
+
+        def gather_codes(s, a, b):
+            nc.vector.tensor_copy(g_codes[s][:, a:b], x_codes[s][:].indirect(offs_t[:, a // 16 : b // 16]))
+
+        def gather_scales(s, a, b):
+            nc.vector.tensor_copy(g_scales[s][:, a:b], x_scales[s][:].indirect(offs_t[:, a // 16 : b // 16]))
+
+        a_bank, r_sb, t_bank, h_codes, h_scales, y_bank = {}, {}, {}, {}, {}, {}
+        y_sb = [keep.tile([P, S], F32, name=f"y_sb{h}") for h in range(2)]
+
+        def first(e):
+            a_ps = psum_a.tile([P, H], F32, name="a_ps")
+            cols = slice(C * e, C * e + C)
+            for s in range(PASSES):
+                g = (e % 2) * 2 + s
+                nc.tensor.matmul_mx(
+                    out=a_ps[:],
+                    lhsT=g_codes[s][:, cols].bitcast(E4M3X4),
+                    lhsT_scale=g_scales[s][:, cols],
+                    rhs=w1_t[e // 2][:, g * 2 * H : (g + 1) * 2 * H].bitcast(E2M1X4),
+                    rhs_scale=w1_pl[:, (2 * e + s) * H : (2 * e + s + 1) * H],
+                    start=(s == 0),
+                    stop=(s == PASSES - 1),
+                )
+            a_bank[e] = a_ps
+
+        def relu(e):
+            r = ring.tile([P, 4, P], F32, name="r")
+            src = a_bank[e][:].rearrange("p (m t) -> p t m", t=4)
+            if e in RELU_ON_VECTOR:
+                nc.vector.tensor_scalar(r[:], src, 0.0, None, MAX)
+            else:
+                nc.scalar.activation(r[:], src, RELU)
+            r_sb[e] = r
+
+        def turn(e):
+            t_ps = psum_t.tile([P, 4, P], F32, name="t_ps")
+            for t in range(4):
+                nc.tensor.transpose(t_ps[:, t, :], r_sb[e][:, t, :], ident[:])
+            t_bank[e] = t_ps
+
+        def square(e):
+            hb = ring.tile([P, P, 4], BF16, name="hb", align_bytes=64)
+            nc.scalar.activation(hb[:], t_bank[e][:].rearrange("p t n -> p n t"), SQUARE)
+            hc = ring.tile([P, P], U32, name="hc", align_bytes=64)
+            hs = ring.tile([P, P], U8, name="hs", align_bytes=64)
+            nc.vector.quantize_mx(out=hc[:].bitcast(E4M3X4), scales=hs[:], in_=hb[:].rearrange("p n t -> p (n t)"))
+            h_codes[e], h_scales[e] = hc, hs
+
+        def second(e):
+            if e % 2 == 0:
+                y_bank[e // 2] = [psum_y.tile([P, 2 * C], F32, name=f"y_ps{h}") for h in range(2)]
+            for h in range(2):
+                nc.tensor.matmul_mx(
+                    out=y_bank[e // 2][h][:, (e % 2) * C : (e % 2 + 1) * C],
+                    lhsT=w2_t[:, e * 2 * N + h * 2 * P : e * 2 * N + (h + 1) * 2 * P].bitcast(E2M1X4),
+                    lhsT_scale=w2_pl[:, e * N + h * P : e * N + (h + 1) * P],
+                    rhs=h_codes[e][:].bitcast(E4M3X4),
+                    rhs_scale=h_scales[e][:],
+                    start=True,
+                    stop=True,
+                )
+
+        def keep_y(pair):
+            for h in range(2):
+                dst = y_sb[h][:, 2 * C * pair : 2 * C * (pair + 1)]
+                if (pair, h) in Y_ON_VECTOR:
+                    nc.vector.tensor_copy(dst, y_bank[pair][h][:])
+                else:
+                    nc.scalar.copy(dst, y_bank[pair][h][:])
+
+        tokens(0)
+        gather_codes(0, 0, 256)
+        gather_scales(0, 0, 256)
+        tokens(1)
+        for e in range(E + 3):
+            if e < 2:
+                a, b = C * e, C * e + C
+                gather_codes(1, a, b)
+                gather_scales(1, a, b)
+            elif e % 2 == 0 and e < E:
+                a, b = C * e, C * e + 2 * C
+                for s in range(PASSES):
+                    gather_codes(s, a, b)
+                    gather_scales(s, a, b)
+            if e < E:
+                first(e)
+                relu(e)
+            if 2 <= e < E + 2:
+                turn(e - 2)
+                square(e - 2)
+            if e >= 3:
+                second(e - 3)
+                if e % 2 == 0:
+                    keep_y((e - 4) // 2)
+
+        half = T // 2
+        for h in range(2):
+            first_prod = keep.tile([P, T], F32, name=f"first_prod{h}")
+            second_prod = keep.tile([P, T], F32, name=f"second_prod{h}")
+            o = keep.tile([P, T], F32, name=f"o{h}")
+            y_h, rows = y_sb[h][:], slice(P * h, P * h + P)
+            nc.vector.tensor_tensor(first_prod[:], y_h.indirect(pos1_t[:]), gates[h][:, 0, :], MULT)
+            cuts = ((0, T),) if h == 0 else ((0, half), (half, T))
+            for a, b in cuts:
+                nc.vector.tensor_tensor(
+                    second_prod[:, a:b], y_h.indirect(pos2_t[:, a // 16 : b // 16]), gates[h][:, 1, a:b], MULT
+                )
+            for a, b in cuts:
+                nc.vector.tensor_tensor(o[:, a:b], first_prod[:, a:b], second_prod[:, a:b], ADD)
+                nc.sync.dma_start(out=out[rows, a:b], in_=o[:, a:b])

@@ -23,8 +23,7 @@ MAX = mybir.AluOpType.max
 RELU = mybir.ActivationFunctionType.Relu
 SQUARE = mybir.ActivationFunctionType.Square
 
-XT = T // 2
-X_SPLIT = {(0, 0): 160, (0, 1): 160, (1, 0): 0, (1, 1): 64}
+X_SPLIT = (320, 288)
 RELU_ON_VECTOR = (6,)
 Y_ON_VECTOR = ((0, 0), (0, 1), (1, 0), (1, 1), (2, 0), (3, 0))
 
@@ -45,44 +44,47 @@ def tile_moe_pln_mlp_relu2_kernel(
         pos1_t = lists.tile([P, T // 16], U16, name="pos1_t")
         pos2_t = lists.tile([P, T // 16], U16, name="pos2_t")
 
-        x_raw = {}
-        w1_pl = keep.tile([P, E * PASSES * H], U8, name="w1_pl", align_bytes=64)
-        w2_pl = keep.tile([P, E * N], U8, name="w2_pl", align_bytes=64)
-        for s in range(PASSES):
-            x_in = xT[512 * s : 512 * s + 512, :].rearrange("(p j) t -> p j t", j=4)
-            for part in range(2):
-                x_part = keep.tile([P, 4, XT], F32, name=f"x_raw{s}{part}")
-                nc.sync.dma_start(out=x_part[:], in_=x_in[:, :, XT * part : XT * part + XT])
-                x_raw[s, part] = x_part
-            if s == 0:
-                nc.sync.dma_start(offs_t[:], offs)
+        x_raw = [keep.tile([P, 4, T], F32, name=f"x_raw{s}") for s in range(PASSES)]
+        nc.sync.dma_start(out=x_raw[0][:], in_=xT[0:512, :].rearrange("(p j) t -> p j t", j=4))
+        nc.sync.dma_start(out=x_raw[1][:], in_=xT[512:1024, :].rearrange("(p j) t -> p j t", j=4))
+        nc.sync.dma_start(offs_t[:], offs)
 
-        nc.vector.memset(w1_pl[:].bitcast(I32), 0)
+        w1_pl = [keep.tile([P, 8 * H], U8, name=f"w1_pl{k}", align_bytes=64) for k in range(2)]
+        w2_pl = keep.tile([P, E * N], U8, name="w2_pl", align_bytes=64)
+        nc.vector.memset(w1_pl[0][:].bitcast(I32), 0)
+        nc.vector.memset(w1_pl[1][:].bitcast(I32), 0)
         nc.vector.memset(w2_pl[:].bitcast(I32), 0)
-        w1_pl_words = w1_pl[:].bitcast(I32).rearrange("p (g i) -> p g i", g=E * PASSES)
-        w2_pl_words = w2_pl[:].bitcast(I32).rearrange("p (g i) -> p g i", g=E)
         w1_sc_words = w1_scales.bitcast(I32).rearrange("e s q i -> q (e s) i")
         w2_sc_words = w2_scales.bitcast(I32).rearrange("e s q i -> q (e s) i")
-        for q in range(4):
-            nc.sync.dma_start(out=w1_pl_words[32 * q : 32 * q + 4], in_=w1_sc_words[4 * q : 4 * q + 4])
+
+        def load_w1_scales(queue, k):
+            words = w1_pl[k][:].bitcast(I32).rearrange("p (g i) -> p g i", g=8)
+            for q in range(4):
+                queue.dma_start(out=words[32 * q : 32 * q + 4], in_=w1_sc_words[4 * q : 4 * q + 4, 8 * k : 8 * k + 8, :])
 
         w1_in = w1_words.bitcast(I32).rearrange("e s p c -> p (e s) c")
-        w1_t = []
-        for pair in range(E // 2):
-            w1_two = keep.tile([P, 4 * 2 * H], U8, name=f"w1_two{pair}", align_bytes=64)
+        w1_t = [keep.tile([P, 4 * 2 * H], U8, name=f"w1_two{k}", align_bytes=64) for k in range(E // 2)]
+        w2_t = keep.tile([P, E * 2 * N], U8, name="w2_t", align_bytes=64)
+
+        def load_w1(pair):
             nc.sync.dma_start(
-                out=w1_two[:].bitcast(I32).rearrange("p (g c) -> p g c", g=4),
+                out=w1_t[pair][:].bitcast(I32).rearrange("p (g c) -> p g c", g=4),
                 in_=w1_in[:, 4 * pair : 4 * pair + 4, :],
             )
-            w1_t.append(w1_two)
-            if pair == 0:
-                for q in range(4):
-                    nc.sync.dma_start(out=w2_pl_words[32 * q : 32 * q + 4], in_=w2_sc_words[4 * q : 4 * q + 4])
-                w2_t = keep.tile([P, E * 2 * N], U8, name="w2_t", align_bytes=64)
-                nc.sync.dma_start(
-                    out=w2_t[:].bitcast(I32).rearrange("p (g c) -> p g c", g=E),
-                    in_=w2_words.bitcast(I32).rearrange("e s p c -> p (e s) c"),
-                )
+
+        load_w1_scales(nc.gpsimd, 0)
+        load_w1(0)
+        load_w1(1)
+        w2_words_sb = w2_pl[:].bitcast(I32).rearrange("p (g i) -> p g i", g=E)
+        for q in range(4):
+            nc.sync.dma_start(out=w2_words_sb[32 * q : 32 * q + 4], in_=w2_sc_words[4 * q : 4 * q + 4])
+        load_w1_scales(nc.sync, 1)
+        nc.sync.dma_start(
+            out=w2_t[:].bitcast(I32).rearrange("p (g c) -> p g c", g=E),
+            in_=w2_words.bitcast(I32).rearrange("e s p c -> p (e s) c"),
+        )
+        load_w1(2)
+        load_w1(3)
         nc.sync.dma_start(pos1_t[:], pos1)
         nc.sync.dma_start(pos2_t[:], pos2)
         gates = []
@@ -106,17 +108,16 @@ def tile_moe_pln_mlp_relu2_kernel(
 
         def tokens(s):
             xb = keep.tile([P, T, 4], BF16, name=f"xb{s}", align_bytes=64)
-            for part in range(2):
-                a, m = XT * part, X_SPLIT[s, part]
-                view = x_raw[s, part][:].rearrange("p j t -> p t j")
-                if m > 0:
-                    nc.vector.tensor_copy(xb[:, a : a + m, :], view[:, 0:m, :])
-                if m < XT:
-                    nc.scalar.copy(xb[:, a + m : a + XT, :], view[:, m:XT, :])
+            half, m = T // 2, X_SPLIT[s]
+            view = x_raw[s][:].rearrange("p j t -> p t j")
+            nc.scalar.copy(xb[:, m:T, :], view[:, m:T, :])
+            nc.vector.tensor_copy(xb[:, 0:half, :], view[:, 0:half, :])
+            nc.vector.tensor_copy(xb[:, half:m, :], view[:, half:m, :])
+            for a in (0, half):
                 nc.vector.quantize_mx(
-                    out=x_codes[s][:, a : a + XT].bitcast(E4M3X4),
-                    scales=x_scales[s][:, a : a + XT],
-                    in_=xb[:, a : a + XT, :].rearrange("p t j -> p (t j)"),
+                    out=x_codes[s][:, a : a + half].bitcast(E4M3X4),
+                    scales=x_scales[s][:, a : a + half],
+                    in_=xb[:, a : a + half, :].rearrange("p t j -> p (t j)"),
                 )
 
         def gather_codes(s, a, b):
@@ -138,7 +139,7 @@ def tile_moe_pln_mlp_relu2_kernel(
                     lhsT=g_codes[s][:, cols].bitcast(E4M3X4),
                     lhsT_scale=g_scales[s][:, cols],
                     rhs=w1_t[e // 2][:, g * 2 * H : (g + 1) * 2 * H].bitcast(E2M1X4),
-                    rhs_scale=w1_pl[:, (2 * e + s) * H : (2 * e + s + 1) * H],
+                    rhs_scale=w1_pl[e // 4][:, (2 * (e % 4) + s) * H : (2 * (e % 4) + s + 1) * H],
                     start=(s == 0),
                     stop=(s == PASSES - 1),
                 )
@@ -215,17 +216,24 @@ def tile_moe_pln_mlp_relu2_kernel(
                     keep_y((e - 4) // 2)
 
         half = T // 2
-        for h in range(2):
-            first_prod = keep.tile([P, T], F32, name=f"first_prod{h}")
-            second_prod = keep.tile([P, T], F32, name=f"second_prod{h}")
-            o = keep.tile([P, T], F32, name=f"o{h}")
-            y_h, rows = y_sb[h][:], slice(P * h, P * h + P)
-            nc.vector.tensor_tensor(first_prod[:], y_h.indirect(pos1_t[:]), gates[h][:, 0, :], MULT)
-            cuts = ((0, T),) if h == 0 else ((0, half), (half, T))
-            for a, b in cuts:
-                nc.vector.tensor_tensor(
-                    second_prod[:, a:b], y_h.indirect(pos2_t[:, a // 16 : b // 16]), gates[h][:, 1, a:b], MULT
-                )
-            for a, b in cuts:
-                nc.vector.tensor_tensor(o[:, a:b], first_prod[:, a:b], second_prod[:, a:b], ADD)
-                nc.sync.dma_start(out=out[rows, a:b], in_=o[:, a:b])
+        prods = [[keep.tile([P, T], F32, name=f"prod{h}{i}") for i in range(2)] for h in range(2)]
+        sums = [keep.tile([P, T], F32, name=f"sum{h}") for h in range(2)]
+
+        def fetch(h, i, a, b):
+            pos_t = (pos1_t, pos2_t)[i]
+            nc.vector.tensor_tensor(
+                prods[h][i][:, a:b], y_sb[h][:].indirect(pos_t[:, a // 16 : b // 16]), gates[h][:, i, a:b], MULT
+            )
+
+        def add(h, a, b):
+            nc.vector.tensor_tensor(sums[h][:, a:b], prods[h][0][:, a:b], prods[h][1][:, a:b], ADD)
+            nc.sync.dma_start(out=out[P * h : P * h + P, a:b], in_=sums[h][:, a:b])
+
+        fetch(0, 0, 0, T)
+        fetch(0, 1, 0, T)
+        fetch(1, 0, 0, T)
+        add(0, 0, T)
+        fetch(1, 1, 0, half)
+        fetch(1, 1, half, T)
+        add(1, 0, half)
+        add(1, half, T)

@@ -23,9 +23,9 @@ MAX = mybir.AluOpType.max
 RELU = mybir.ActivationFunctionType.Relu
 SQUARE = mybir.ActivationFunctionType.Square
 
-X_SPLIT = (320, 288)
-RELU_ON_VECTOR = (6,)
-Y_ON_VECTOR = ((0, 0), (0, 1), (1, 0), (1, 1), (2, 0), (3, 0))
+X_ON_VECTOR = ((128, 256,), (0, 0,))
+RELU_ON_VECTOR = (6, 7,)
+Y_ON_VECTOR = ((2, 1),)
 
 
 def tile_moe_pln_mlp_relu2_kernel(
@@ -35,9 +35,9 @@ def tile_moe_pln_mlp_relu2_kernel(
     with ExitStack() as ctx:
         lists = ctx.enter_context(tc.tile_pool(name="lists", bufs=1))
         keep = ctx.enter_context(tc.tile_pool(name="keep", bufs=1))
-        ring = ctx.enter_context(tc.tile_pool(name="ring", bufs=3))
-        psum_a = ctx.enter_context(tc.psum_pool(name="psum_a", bufs=3))
-        psum_t = ctx.enter_context(tc.psum_pool(name="psum_t", bufs=3))
+        ring = ctx.enter_context(tc.tile_pool(name="ring", bufs=4))
+        psum_a = ctx.enter_context(tc.psum_pool(name="psum_a", bufs=4))
+        psum_t = ctx.enter_context(tc.psum_pool(name="psum_t", bufs=2))
         psum_y = ctx.enter_context(tc.psum_pool(name="psum_y", bufs=1))
 
         offs_t = lists.tile([P, S // 16], U16, name="offs_t")
@@ -46,21 +46,19 @@ def tile_moe_pln_mlp_relu2_kernel(
 
         x_raw = [keep.tile([P, 4, T], F32, name=f"x_raw{s}") for s in range(PASSES)]
         nc.sync.dma_start(out=x_raw[0][:], in_=xT[0:512, :].rearrange("(p j) t -> p j t", j=4))
-        nc.sync.dma_start(out=x_raw[1][:], in_=xT[512:1024, :].rearrange("(p j) t -> p j t", j=4))
         nc.sync.dma_start(offs_t[:], offs)
+        nc.sync.dma_start(out=x_raw[1][:], in_=xT[512:1024, :].rearrange("(p j) t -> p j t", j=4))
 
-        w1_pl = [keep.tile([P, 8 * H], U8, name=f"w1_pl{k}", align_bytes=64) for k in range(2)]
+        w1_pl = keep.tile([P, E * PASSES * H], U8, name="w1_pl", align_bytes=64)
         w2_pl = keep.tile([P, E * N], U8, name="w2_pl", align_bytes=64)
-        nc.vector.memset(w1_pl[0][:].bitcast(I32), 0)
-        nc.vector.memset(w1_pl[1][:].bitcast(I32), 0)
+        nc.vector.memset(w1_pl[:].bitcast(I32), 0)
         nc.vector.memset(w2_pl[:].bitcast(I32), 0)
-        w1_sc_words = w1_scales.bitcast(I32).rearrange("e s q i -> q (e s) i")
-        w2_sc_words = w2_scales.bitcast(I32).rearrange("e s q i -> q (e s) i")
 
-        def load_w1_scales(queue, k):
-            words = w1_pl[k][:].bitcast(I32).rearrange("p (g i) -> p g i", g=8)
+        def load_scales(plane, scales, groups):
+            plane_words = plane[:].bitcast(I32).rearrange("p (g i) -> p g i", g=groups)
+            scale_words = scales.bitcast(I32).rearrange("e s q i -> q (e s) i")
             for q in range(4):
-                queue.dma_start(out=words[32 * q : 32 * q + 4], in_=w1_sc_words[4 * q : 4 * q + 4, 8 * k : 8 * k + 8, :])
+                nc.sync.dma_start(out=plane_words[32 * q : 32 * q + 4], in_=scale_words[4 * q : 4 * q + 4])
 
         w1_in = w1_words.bitcast(I32).rearrange("e s p c -> p (e s) c")
         w1_t = [keep.tile([P, 4 * 2 * H], U8, name=f"w1_two{k}", align_bytes=64) for k in range(E // 2)]
@@ -72,13 +70,10 @@ def tile_moe_pln_mlp_relu2_kernel(
                 in_=w1_in[:, 4 * pair : 4 * pair + 4, :],
             )
 
-        load_w1_scales(nc.gpsimd, 0)
+        load_scales(w1_pl, w1_scales, E * PASSES)
         load_w1(0)
         load_w1(1)
-        w2_words_sb = w2_pl[:].bitcast(I32).rearrange("p (g i) -> p g i", g=E)
-        for q in range(4):
-            nc.sync.dma_start(out=w2_words_sb[32 * q : 32 * q + 4], in_=w2_sc_words[4 * q : 4 * q + 4])
-        load_w1_scales(nc.sync, 1)
+        load_scales(w2_pl, w2_scales, E)
         nc.sync.dma_start(
             out=w2_t[:].bitcast(I32).rearrange("p (g c) -> p g c", g=E),
             in_=w2_words.bitcast(I32).rearrange("e s p c -> p (e s) c"),
@@ -108,16 +103,19 @@ def tile_moe_pln_mlp_relu2_kernel(
 
         def tokens(s):
             xb = keep.tile([P, T, 4], BF16, name=f"xb{s}", align_bytes=64)
-            half, m = T // 2, X_SPLIT[s]
+            half = T // 2
             view = x_raw[s][:].rearrange("p j t -> p t j")
-            nc.scalar.copy(xb[:, m:T, :], view[:, m:T, :])
-            nc.vector.tensor_copy(xb[:, 0:half, :], view[:, 0:half, :])
-            nc.vector.tensor_copy(xb[:, half:m, :], view[:, half:m, :])
-            for a in (0, half):
+            for part in range(2):
+                a, b = half * part, half * part + half
+                m = a + X_ON_VECTOR[s][part]
+                if m > a:
+                    nc.vector.tensor_copy(xb[:, a:m, :], view[:, a:m, :])
+                if m < b:
+                    nc.scalar.copy(xb[:, m:b, :], view[:, m:b, :])
                 nc.vector.quantize_mx(
-                    out=x_codes[s][:, a : a + half].bitcast(E4M3X4),
-                    scales=x_scales[s][:, a : a + half],
-                    in_=xb[:, a : a + half, :].rearrange("p t j -> p (t j)"),
+                    out=x_codes[s][:, a:b].bitcast(E4M3X4),
+                    scales=x_scales[s][:, a:b],
+                    in_=xb[:, a:b, :].rearrange("p t j -> p (t j)"),
                 )
 
         def gather_codes(s, a, b):
@@ -126,7 +124,7 @@ def tile_moe_pln_mlp_relu2_kernel(
         def gather_scales(s, a, b):
             nc.vector.tensor_copy(g_scales[s][:, a:b], x_scales[s][:].indirect(offs_t[:, a // 16 : b // 16]))
 
-        a_bank, r_sb, t_bank, h_codes, h_scales, y_bank = {}, {}, {}, {}, {}, {}
+        a_bank, r_sb, t_bank, h_bf16, h_codes, h_scales, y_bank = {}, {}, {}, {}, {}, {}, {}
         y_sb = [keep.tile([P, S], F32, name=f"y_sb{h}") for h in range(2)]
 
         def first(e):
@@ -139,7 +137,7 @@ def tile_moe_pln_mlp_relu2_kernel(
                     lhsT=g_codes[s][:, cols].bitcast(E4M3X4),
                     lhsT_scale=g_scales[s][:, cols],
                     rhs=w1_t[e // 2][:, g * 2 * H : (g + 1) * 2 * H].bitcast(E2M1X4),
-                    rhs_scale=w1_pl[e // 4][:, (2 * (e % 4) + s) * H : (2 * (e % 4) + s + 1) * H],
+                    rhs_scale=w1_pl[:, (2 * e + s) * H : (2 * e + s + 1) * H],
                     start=(s == 0),
                     stop=(s == PASSES - 1),
                 )
@@ -163,9 +161,12 @@ def tile_moe_pln_mlp_relu2_kernel(
         def square(e):
             hb = ring.tile([P, P, 4], BF16, name="hb", align_bytes=64)
             nc.scalar.activation(hb[:], t_bank[e][:].rearrange("p t n -> p n t"), SQUARE)
+            h_bf16[e] = hb
+
+        def quantise_h(e):
             hc = ring.tile([P, P], U32, name="hc", align_bytes=64)
             hs = ring.tile([P, P], U8, name="hs", align_bytes=64)
-            nc.vector.quantize_mx(out=hc[:].bitcast(E4M3X4), scales=hs[:], in_=hb[:].rearrange("p n t -> p (n t)"))
+            nc.vector.quantize_mx(out=hc[:].bitcast(E4M3X4), scales=hs[:], in_=h_bf16[e][:].rearrange("p n t -> p (n t)"))
             h_codes[e], h_scales[e] = hc, hs
 
         def second(e):
@@ -191,29 +192,42 @@ def tile_moe_pln_mlp_relu2_kernel(
                     nc.scalar.copy(dst, y_bank[pair][h][:])
 
         tokens(0)
-        gather_codes(0, 0, 256)
-        gather_scales(0, 0, 256)
+        gather_codes(0, 0 * C, 2 * C)
+        gather_scales(0, 0 * C, 2 * C)
         tokens(1)
-        for e in range(E + 3):
-            if e < 2:
-                a, b = C * e, C * e + C
-                gather_codes(1, a, b)
-                gather_scales(1, a, b)
-            elif e % 2 == 0 and e < E:
-                a, b = C * e, C * e + 2 * C
-                for s in range(PASSES):
-                    gather_codes(s, a, b)
-                    gather_scales(s, a, b)
+        for e in range(E + 7):
+            if e == 0:
+                gather_scales(1, 1 * C, 3 * C)
+                gather_codes(1, 0 * C, 1 * C)
+                gather_scales(0, 2 * C, 5 * C)
+                gather_scales(1, 0 * C, 1 * C)
+            if e == 1:
+                gather_codes(0, 2 * C, 5 * C)
+                gather_codes(1, 1 * C, 4 * C)
+            if e == 2:
+                gather_codes(0, 7 * C, 8 * C)
+                gather_scales(0, 6 * C, 8 * C)
+                gather_scales(1, 3 * C, 4 * C)
+                gather_scales(1, 4 * C, 5 * C)
+                gather_scales(0, 5 * C, 6 * C)
+                gather_codes(1, 7 * C, 8 * C)
+            if e == 3:
+                gather_codes(0, 5 * C, 7 * C)
+                gather_codes(1, 4 * C, 7 * C)
+            if e == 5:
+                gather_scales(1, 5 * C, 8 * C)
             if e < E:
                 first(e)
                 relu(e)
             if 2 <= e < E + 2:
                 turn(e - 2)
                 square(e - 2)
-            if e >= 3:
-                second(e - 3)
-                if e % 2 == 0:
-                    keep_y((e - 4) // 2)
+            if 3 <= e < E + 3:
+                quantise_h(e - 3)
+            if 5 <= e < E + 5:
+                second(e - 5)
+            if e >= 7 and (e - 7) % 2 == 1:
+                keep_y((e - 7) // 2)
 
         half = T // 2
         prods = [[keep.tile([P, T], F32, name=f"prod{h}{i}") for i in range(2)] for h in range(2)]

@@ -23,9 +23,9 @@ MAX = mybir.AluOpType.max
 RELU = mybir.ActivationFunctionType.Relu
 SQUARE = mybir.ActivationFunctionType.Square
 
-X_ON_VECTOR = ((128, 256,), (0, 0,))
-RELU_ON_VECTOR = (6, 7,)
-Y_ON_VECTOR = ((2, 1),)
+X_ON_VECTOR = ((160, 160,), (64, 128,))
+RELU_ON_VECTOR = (7,)
+Y_ON_VECTOR = ((0, 1), (1, 1), (3, 1),)
 
 
 def tile_moe_pln_mlp_relu2_kernel(
@@ -36,8 +36,8 @@ def tile_moe_pln_mlp_relu2_kernel(
         lists = ctx.enter_context(tc.tile_pool(name="lists", bufs=1))
         keep = ctx.enter_context(tc.tile_pool(name="keep", bufs=1))
         ring = ctx.enter_context(tc.tile_pool(name="ring", bufs=4))
-        psum_a = ctx.enter_context(tc.psum_pool(name="psum_a", bufs=4))
-        psum_t = ctx.enter_context(tc.psum_pool(name="psum_t", bufs=2))
+        psum_a = ctx.enter_context(tc.psum_pool(name="psum_a", bufs=3))
+        psum_t = ctx.enter_context(tc.psum_pool(name="psum_t", bufs=3))
         psum_y = ctx.enter_context(tc.psum_pool(name="psum_y", bufs=1))
 
         offs_t = lists.tile([P, S // 16], U16, name="offs_t")
@@ -49,14 +49,15 @@ def tile_moe_pln_mlp_relu2_kernel(
         nc.sync.dma_start(offs_t[:], offs)
         nc.sync.dma_start(out=x_raw[1][:], in_=xT[512:1024, :].rearrange("(p j) t -> p j t", j=4))
 
-        w1_pl = keep.tile([P, E * PASSES * H], U8, name="w1_pl", align_bytes=64)
+        w1_pl = [keep.tile([P, 8 * H], U8, name=f"w1_pl{k}", align_bytes=64) for k in range(2)]
         w2_pl = keep.tile([P, E * N], U8, name="w2_pl", align_bytes=64)
-        nc.vector.memset(w1_pl[:].bitcast(I32), 0)
-        nc.vector.memset(w2_pl[:].bitcast(I32), 0)
+        nc.vector.memset(w1_pl[0][:].bitcast(I32), 0)
+        nc.gpsimd.memset(w1_pl[1][:].bitcast(I32), 0)
+        nc.gpsimd.memset(w2_pl[:].bitcast(I32), 0)
 
-        def load_scales(plane, scales, groups):
+        def load_scales(plane, scales, groups, start):
             plane_words = plane[:].bitcast(I32).rearrange("p (g i) -> p g i", g=groups)
-            scale_words = scales.bitcast(I32).rearrange("e s q i -> q (e s) i")
+            scale_words = scales.bitcast(I32).rearrange("e s q i -> q (e s) i")[:, start : start + groups, :]
             for q in range(4):
                 nc.sync.dma_start(out=plane_words[32 * q : 32 * q + 4], in_=scale_words[4 * q : 4 * q + 4])
 
@@ -70,15 +71,16 @@ def tile_moe_pln_mlp_relu2_kernel(
                 in_=w1_in[:, 4 * pair : 4 * pair + 4, :],
             )
 
-        load_scales(w1_pl, w1_scales, E * PASSES)
         load_w1(0)
+        load_scales(w1_pl[0], w1_scales, 8, 0)
         load_w1(1)
-        load_scales(w2_pl, w2_scales, E)
+        load_scales(w1_pl[1], w1_scales, 8, 8)
+        load_w1(2)
+        load_scales(w2_pl, w2_scales, E, 0)
         nc.sync.dma_start(
             out=w2_t[:].bitcast(I32).rearrange("p (g c) -> p g c", g=E),
             in_=w2_words.bitcast(I32).rearrange("e s p c -> p (e s) c"),
         )
-        load_w1(2)
         load_w1(3)
         nc.sync.dma_start(pos1_t[:], pos1)
         nc.sync.dma_start(pos2_t[:], pos2)
@@ -104,14 +106,15 @@ def tile_moe_pln_mlp_relu2_kernel(
         def tokens(s):
             xb = keep.tile([P, T, 4], BF16, name=f"xb{s}", align_bytes=64)
             half = T // 2
-            view = x_raw[s][:].rearrange("p j t -> p t j")
+            view = x_raw[s][:].rearrange("p j (c i) -> p c j i", i=4)
+            dst = xb[:].rearrange("p (c i) j -> p c j i", i=4)
             for part in range(2):
                 a, b = half * part, half * part + half
                 m = a + X_ON_VECTOR[s][part]
                 if m > a:
-                    nc.vector.tensor_copy(xb[:, a:m, :], view[:, a:m, :])
+                    nc.vector.tensor_copy(dst[:, a // 4 : m // 4], view[:, a // 4 : m // 4])
                 if m < b:
-                    nc.scalar.copy(xb[:, m:b, :], view[:, m:b, :])
+                    nc.scalar.copy(dst[:, m // 4 : b // 4], view[:, m // 4 : b // 4])
                 nc.vector.quantize_mx(
                     out=x_codes[s][:, a:b].bitcast(E4M3X4),
                     scales=x_scales[s][:, a:b],
@@ -137,7 +140,7 @@ def tile_moe_pln_mlp_relu2_kernel(
                     lhsT=g_codes[s][:, cols].bitcast(E4M3X4),
                     lhsT_scale=g_scales[s][:, cols],
                     rhs=w1_t[e // 2][:, g * 2 * H : (g + 1) * 2 * H].bitcast(E2M1X4),
-                    rhs_scale=w1_pl[:, (2 * e + s) * H : (2 * e + s + 1) * H],
+                    rhs_scale=w1_pl[e // 4][:, (2 * (e % 4) + s) * H : (2 * (e % 4) + s + 1) * H],
                     start=(s == 0),
                     stop=(s == PASSES - 1),
                 )
@@ -145,11 +148,12 @@ def tile_moe_pln_mlp_relu2_kernel(
 
         def relu(e):
             r = ring.tile([P, 4, P], F32, name="r")
-            src = a_bank[e][:].rearrange("p (m t) -> p t m", t=4)
+            src = a_bank[e][:].rearrange("p (m t) -> p m t", t=4)
+            dst = r[:].rearrange("p t m -> p m t")
             if e in RELU_ON_VECTOR:
-                nc.vector.tensor_scalar(r[:], src, 0.0, None, MAX)
+                nc.vector.tensor_scalar(dst, src, 0.0, None, MAX)
             else:
-                nc.scalar.activation(r[:], src, RELU)
+                nc.scalar.activation(dst, src, RELU)
             r_sb[e] = r
 
         def turn(e):
@@ -192,38 +196,41 @@ def tile_moe_pln_mlp_relu2_kernel(
                     nc.scalar.copy(dst, y_bank[pair][h][:])
 
         tokens(0)
-        gather_codes(0, 0 * C, 2 * C)
-        gather_scales(0, 0 * C, 2 * C)
+        gather_codes(0, 0 * C, 3 * C)
+        gather_codes(0, 3 * C, 4 * C)
         tokens(1)
         for e in range(E + 7):
             if e == 0:
-                gather_scales(1, 1 * C, 3 * C)
-                gather_codes(1, 0 * C, 1 * C)
-                gather_scales(0, 2 * C, 5 * C)
                 gather_scales(1, 0 * C, 1 * C)
+                gather_codes(1, 0 * C, 1 * C)
+                gather_scales(1, 1 * C, 3 * C)
+                gather_codes(1, 1 * C, 3 * C)
+                gather_scales(0, 0 * C, 3 * C)
+                gather_codes(0, 4 * C, 5 * C)
             if e == 1:
-                gather_codes(0, 2 * C, 5 * C)
-                gather_codes(1, 1 * C, 4 * C)
-            if e == 2:
-                gather_codes(0, 7 * C, 8 * C)
                 gather_scales(0, 6 * C, 8 * C)
                 gather_scales(1, 3 * C, 4 * C)
+                gather_scales(0, 3 * C, 6 * C)
                 gather_scales(1, 4 * C, 5 * C)
-                gather_scales(0, 5 * C, 6 * C)
-                gather_codes(1, 7 * C, 8 * C)
             if e == 3:
-                gather_codes(0, 5 * C, 7 * C)
-                gather_codes(1, 4 * C, 7 * C)
+                gather_codes(1, 3 * C, 4 * C)
+                gather_codes(1, 4 * C, 5 * C)
+            if e == 4:
+                gather_codes(0, 5 * C, 6 * C)
             if e == 5:
+                gather_codes(1, 5 * C, 8 * C)
                 gather_scales(1, 5 * C, 8 * C)
+            if e == 6:
+                gather_codes(0, 6 * C, 7 * C)
+                gather_codes(0, 7 * C, 8 * C)
             if e < E:
                 first(e)
                 relu(e)
             if 2 <= e < E + 2:
                 turn(e - 2)
                 square(e - 2)
-            if 3 <= e < E + 3:
-                quantise_h(e - 3)
+            if 4 <= e < E + 4:
+                quantise_h(e - 4)
             if 5 <= e < E + 5:
                 second(e - 5)
             if e >= 7 and (e - 7) % 2 == 1:

@@ -6,7 +6,13 @@ from concourse.masks import make_identity
 K, T, E, C, H, N = 1024, 512, 8, 128, 512, 256
 S = E * C
 P = 128
-PASSES = K // 512
+PACK = 4
+PASS_K = P * PACK
+PASSES = K // PASS_K
+HALVES = N // P
+FP4_BYTES = 2
+PAIRS = E // 2
+
 FLOPS = 2 * S * (K * H + H * N)
 
 F32 = mybir.dt.float32
@@ -23,9 +29,17 @@ MAX = mybir.AluOpType.max
 RELU = mybir.ActivationFunctionType.Relu
 SQUARE = mybir.ActivationFunctionType.Square
 
-X_ON_VECTOR = ((160, 160,), (64, 128,))
-RELU_ON_VECTOR = (7,)
-Y_ON_VECTOR = ((0, 1), (1, 1), (3, 1),)
+X_ON_VECTOR = ((160, 160), (64, 128))
+RELU_ON_VECTOR = (6, 7)
+Y_ON_VECTOR = ((1, 1), (2, 1), (3, 1))
+
+EARLY_GROUPS = ((0, 1), (1, 3))
+LATE_GROUPS = ((3, 5), (5, 8))
+LATE = LATE_GROUPS[0][0]
+
+TURN_LAG = 2
+SECOND_LAG = 5
+KEEP_LAG = 7
 
 
 def tile_moe_pln_mlp_relu2_kernel(
@@ -35,60 +49,70 @@ def tile_moe_pln_mlp_relu2_kernel(
     with ExitStack() as ctx:
         lists = ctx.enter_context(tc.tile_pool(name="lists", bufs=1))
         keep = ctx.enter_context(tc.tile_pool(name="keep", bufs=1))
+        turns = ctx.enter_context(tc.tile_pool(name="turns", bufs=1))
         ring = ctx.enter_context(tc.tile_pool(name="ring", bufs=4))
-        psum_a = ctx.enter_context(tc.psum_pool(name="psum_a", bufs=3))
-        psum_t = ctx.enter_context(tc.psum_pool(name="psum_t", bufs=3))
+        psum_a = ctx.enter_context(tc.psum_pool(name="psum_a", bufs=4))
+        psum_t = ctx.enter_context(tc.psum_pool(name="psum_t", bufs=2))
         psum_y = ctx.enter_context(tc.psum_pool(name="psum_y", bufs=1))
 
-        offs_t = lists.tile([P, S // 16], U16, name="offs_t")
-        pos1_t = lists.tile([P, T // 16], U16, name="pos1_t")
-        pos2_t = lists.tile([P, T // 16], U16, name="pos2_t")
+        offs_sb = lists.tile([P, S // 16], U16, name="offs_sb")
+        pos1_sb = lists.tile([P, T // 16], U16, name="pos1_sb")
+        pos2_sb = lists.tile([P, T // 16], U16, name="pos2_sb")
 
-        x_raw = [keep.tile([P, 4, T], F32, name=f"x_raw{s}") for s in range(PASSES)]
-        nc.sync.dma_start(out=x_raw[0][:], in_=xT[0:512, :].rearrange("(p j) t -> p j t", j=4))
-        nc.sync.dma_start(offs_t[:], offs)
-        nc.sync.dma_start(out=x_raw[1][:], in_=xT[512:1024, :].rearrange("(p j) t -> p j t", j=4))
+        x_raw = [
+            turns.tile([P, PACK, T], F32, name=f"x_raw{s}", tag=f"x_raw{s}", align_bytes=64) for s in range(PASSES)
+        ]
 
-        w1_pl = [keep.tile([P, 8 * H], U8, name=f"w1_pl{k}", align_bytes=64) for k in range(2)]
-        w2_pl = keep.tile([P, E * N], U8, name="w2_pl", align_bytes=64)
-        nc.vector.memset(w1_pl[0][:].bitcast(I32), 0)
-        nc.gpsimd.memset(w1_pl[1][:].bitcast(I32), 0)
-        nc.gpsimd.memset(w2_pl[:].bitcast(I32), 0)
+        def load_x(s):
+            rows = xT[PASS_K * s : PASS_K * s + PASS_K, :]
+            nc.sync.dma_start(out=x_raw[s][:], in_=rows.rearrange("(p j) t -> p j t", j=PACK))
 
-        def load_scales(plane, scales, groups, start):
-            plane_words = plane[:].bitcast(I32).rearrange("p (g i) -> p g i", g=groups)
-            scale_words = scales.bitcast(I32).rearrange("e s q i -> q (e s) i")[:, start : start + groups, :]
+        load_x(0)
+        nc.sync.dma_start(offs_sb[:], offs)
+        load_x(1)
+
+        quad = 4 * PASSES
+        w1_sc = [keep.tile([P, quad * H], U8, name=f"w1_sc{k}", align_bytes=64) for k in range(2)]
+        w2_sc = keep.tile([P, E * N], U8, name="w2_sc", align_bytes=64)
+        nc.vector.memset(w1_sc[0][:].bitcast(I32), 0)
+        nc.gpsimd.memset(w1_sc[1][:].bitcast(I32), 0)
+        nc.gpsimd.memset(w2_sc[:].bitcast(I32), 0)
+
+        def load_scales(tile, scales, count, start):
+            dst = tile[:].bitcast(I32).rearrange("p (g i) -> p g i", g=count)
+            src = scales.bitcast(I32).rearrange("e s q i -> q (e s) i")[:, start : start + count, :]
             for q in range(4):
-                nc.sync.dma_start(out=plane_words[32 * q : 32 * q + 4], in_=scale_words[4 * q : 4 * q + 4])
+                nc.sync.dma_start(out=dst[32 * q : 32 * q + 4], in_=src[4 * q : 4 * q + 4])
 
-        w1_in = w1_words.bitcast(I32).rearrange("e s p c -> p (e s) c")
-        w1_t = [keep.tile([P, 4 * 2 * H], U8, name=f"w1_two{k}", align_bytes=64) for k in range(E // 2)]
-        w2_t = keep.tile([P, E * 2 * N], U8, name="w2_t", align_bytes=64)
+        pair_passes = 2 * PASSES
+        w1_sb = [keep.tile([P, pair_passes * FP4_BYTES * H], U8, name=f"w1_sb{k}", align_bytes=64) for k in range(PAIRS)]
+        w2_sb = keep.tile([P, E * FP4_BYTES * N], U8, name="w2_sb", align_bytes=64)
 
         def load_w1(pair):
+            src = w1_words.bitcast(I32).rearrange("e s p c -> p (e s) c")
             nc.sync.dma_start(
-                out=w1_t[pair][:].bitcast(I32).rearrange("p (g c) -> p g c", g=4),
-                in_=w1_in[:, 4 * pair : 4 * pair + 4, :],
+                out=w1_sb[pair][:].bitcast(I32).rearrange("p (g c) -> p g c", g=pair_passes),
+                in_=src[:, pair_passes * pair : pair_passes * pair + pair_passes, :],
             )
 
         load_w1(0)
-        load_scales(w1_pl[0], w1_scales, 8, 0)
+        load_scales(w1_sc[0], w1_scales, quad, 0)
         load_w1(1)
-        load_scales(w1_pl[1], w1_scales, 8, 8)
+        load_scales(w1_sc[1], w1_scales, quad, quad)
         load_w1(2)
-        load_scales(w2_pl, w2_scales, E, 0)
+        load_scales(w2_sc, w2_scales, E, 0)
         nc.sync.dma_start(
-            out=w2_t[:].bitcast(I32).rearrange("p (g c) -> p g c", g=E),
+            out=w2_sb[:].bitcast(I32).rearrange("p (g c) -> p g c", g=E),
             in_=w2_words.bitcast(I32).rearrange("e s p c -> p (e s) c"),
         )
         load_w1(3)
-        nc.sync.dma_start(pos1_t[:], pos1)
-        nc.sync.dma_start(pos2_t[:], pos2)
-        gates = []
-        for h in range(2):
-            gate_h = keep.tile([P, 2, T], F32, name=f"gate_h{h}")
-            nc.sync.dma_start(out=gate_h[:], in_=gate[:, P * h : P * h + P, :].rearrange("g n t -> n g t"))
-            gates.append(gate_h)
+        nc.sync.dma_start(pos1_sb[:], pos1)
+        nc.sync.dma_start(pos2_sb[:], pos2)
+        gate_sb = []
+        for h in range(HALVES):
+            gate_half = keep.tile([P, 2, T], F32, name=f"gate_half{h}")
+            nc.sync.dma_start(out=gate_half[:], in_=gate[:, P * h : P * h + P, :].rearrange("g n t -> n g t"))
+            gate_sb.append(gate_half)
 
         warm = keep.tile([P, 1], F32, name="warm")
         nc.gpsimd.memset(warm[:], 0.0)
@@ -100,87 +124,101 @@ def tile_moe_pln_mlp_relu2_kernel(
         make_identity(nc, ident[:])
 
         x_codes = [keep.tile([P, T], U32, name=f"x_codes{s}", align_bytes=64) for s in range(PASSES)]
-        g_codes = [keep.tile([P, S], U32, name=f"g_codes{s}", align_bytes=64) for s in range(PASSES)]
-        g_scales = [keep.tile([P, S], U8, name=f"g_scales{s}", align_bytes=64) for s in range(PASSES)]
+        g_codes = {
+            (0, 0): keep.tile([P, LATE * C], U32, name="g_codes0_early", align_bytes=64),
+            (1, 0): keep.tile([P, S], U32, name="g_codes1", align_bytes=64),
+        }
+        g_scales = {
+            (0, 0): keep.tile([P, LATE * C], U8, name="g_scales0_early", align_bytes=64),
+            (1, 0): keep.tile([P, S], U8, name="g_scales1", align_bytes=64),
+        }
 
-        def tokens(s):
-            xb = keep.tile([P, T, 4], BF16, name=f"xb{s}", align_bytes=64)
+        def slots(tiles, s, a, b):
+            late = s == 0 and a >= LATE * C
+            start = LATE * C if late else 0
+            return tiles[s, int(late)][:, a - start : b - start]
+
+        def quantise_tokens(s):
+            x_bf16 = turns.tile([P, T, PACK], BF16, name=f"x_bf16_{s}", tag=f"x_bf16_{s}", align_bytes=64)
             half = T // 2
-            view = x_raw[s][:].rearrange("p j (c i) -> p c j i", i=4)
-            dst = xb[:].rearrange("p (c i) j -> p c j i", i=4)
+            src = x_raw[s][:].rearrange("p j (c i) -> p c j i", i=4)
+            dst = x_bf16[:].rearrange("p (c i) j -> p c j i", i=4)
             for part in range(2):
                 a, b = half * part, half * part + half
                 m = a + X_ON_VECTOR[s][part]
-                if m > a:
-                    nc.vector.tensor_copy(dst[:, a // 4 : m // 4], view[:, a // 4 : m // 4])
-                if m < b:
-                    nc.scalar.copy(dst[:, m // 4 : b // 4], view[:, m // 4 : b // 4])
+                nc.vector.tensor_copy(dst[:, a // 4 : m // 4], src[:, a // 4 : m // 4])
+                nc.scalar.copy(dst[:, m // 4 : b // 4], src[:, m // 4 : b // 4])
                 nc.vector.quantize_mx(
                     out=x_codes[s][:, a:b].bitcast(E4M3X4),
                     scales=x_scales[s][:, a:b],
-                    in_=xb[:, a:b, :].rearrange("p t j -> p (t j)"),
+                    in_=x_bf16[:, a:b, :].rearrange("p t j -> p (t j)"),
                 )
 
-        def gather_codes(s, a, b):
-            nc.vector.tensor_copy(g_codes[s][:, a:b], x_codes[s][:].indirect(offs_t[:, a // 16 : b // 16]))
+        def gather_codes(s, group):
+            a, b = group[0] * C, group[1] * C
+            nc.vector.tensor_copy(slots(g_codes, s, a, b), x_codes[s][:].indirect(offs_sb[:, a // 16 : b // 16]))
 
-        def gather_scales(s, a, b):
-            nc.vector.tensor_copy(g_scales[s][:, a:b], x_scales[s][:].indirect(offs_t[:, a // 16 : b // 16]))
+        def gather_scales(s, group):
+            a, b = group[0] * C, group[1] * C
+            nc.vector.tensor_copy(slots(g_scales, s, a, b), x_scales[s][:].indirect(offs_sb[:, a // 16 : b // 16]))
 
-        a_bank, r_sb, t_bank, h_bf16, h_codes, h_scales, y_bank = {}, {}, {}, {}, {}, {}, {}
-        y_sb = [keep.tile([P, S], F32, name=f"y_sb{h}") for h in range(2)]
+        a_bank, relu_sb, turned, h_bf16, h_codes, h_scales, y_bank = {}, {}, {}, {}, {}, {}, {}
+        y_sb = [keep.tile([P, S], F32, name=f"y_sb{h}") for h in range(HALVES)]
 
-        def first(e):
+        def first_product(e):
             a_ps = psum_a.tile([P, H], F32, name="a_ps")
-            cols = slice(C * e, C * e + C)
             for s in range(PASSES):
-                g = (e % 2) * 2 + s
+                in_pair = (e % 2) * PASSES + s
+                in_quad = (e % 4) * PASSES + s
                 nc.tensor.matmul_mx(
                     out=a_ps[:],
-                    lhsT=g_codes[s][:, cols].bitcast(E4M3X4),
-                    lhsT_scale=g_scales[s][:, cols],
-                    rhs=w1_t[e // 2][:, g * 2 * H : (g + 1) * 2 * H].bitcast(E2M1X4),
-                    rhs_scale=w1_pl[e // 4][:, (2 * (e % 4) + s) * H : (2 * (e % 4) + s + 1) * H],
+                    lhsT=slots(g_codes, s, C * e, C * e + C).bitcast(E4M3X4),
+                    lhsT_scale=slots(g_scales, s, C * e, C * e + C),
+                    rhs=w1_sb[e // 2][:, in_pair * FP4_BYTES * H : (in_pair + 1) * FP4_BYTES * H].bitcast(E2M1X4),
+                    rhs_scale=w1_sc[e // 4][:, in_quad * H : (in_quad + 1) * H],
                     start=(s == 0),
                     stop=(s == PASSES - 1),
                 )
             a_bank[e] = a_ps
 
         def relu(e):
-            r = ring.tile([P, 4, P], F32, name="r")
-            src = a_bank[e][:].rearrange("p (m t) -> p m t", t=4)
+            r = ring.tile([P, PACK, P], F32, name="r")
+            src = a_bank[e][:].rearrange("p (m t) -> p m t", t=PACK)
             dst = r[:].rearrange("p t m -> p m t")
             if e in RELU_ON_VECTOR:
                 nc.vector.tensor_scalar(dst, src, 0.0, None, MAX)
             else:
                 nc.scalar.activation(dst, src, RELU)
-            r_sb[e] = r
+            relu_sb[e] = r
 
         def turn(e):
-            t_ps = psum_t.tile([P, 4, P], F32, name="t_ps")
-            for t in range(4):
-                nc.tensor.transpose(t_ps[:, t, :], r_sb[e][:, t, :], ident[:])
-            t_bank[e] = t_ps
+            t_ps = psum_t.tile([P, PACK, P], F32, name="t_ps")
+            for t in range(PACK):
+                nc.tensor.transpose(t_ps[:, t, :], relu_sb[e][:, t, :], ident[:])
+            turned[e] = t_ps
 
         def square(e):
-            hb = ring.tile([P, P, 4], BF16, name="hb", align_bytes=64)
-            nc.scalar.activation(hb[:], t_bank[e][:].rearrange("p t n -> p n t"), SQUARE)
-            h_bf16[e] = hb
+            h_sb = ring.tile([P, P, PACK], BF16, name="h_sb", align_bytes=64)
+            nc.scalar.activation(h_sb[:], turned[e][:].rearrange("p t c -> p c t"), SQUARE)
+            h_bf16[e] = h_sb
 
         def quantise_h(e):
-            hc = ring.tile([P, P], U32, name="hc", align_bytes=64)
-            hs = ring.tile([P, P], U8, name="hs", align_bytes=64)
-            nc.vector.quantize_mx(out=hc[:].bitcast(E4M3X4), scales=hs[:], in_=h_bf16[e][:].rearrange("p n t -> p (n t)"))
-            h_codes[e], h_scales[e] = hc, hs
+            codes = ring.tile([P, P], U32, name="codes", align_bytes=64)
+            scales = ring.tile([P, P], U8, name="scales", align_bytes=64)
+            nc.vector.quantize_mx(
+                out=codes[:].bitcast(E4M3X4), scales=scales[:], in_=h_bf16[e][:].rearrange("p c t -> p (c t)")
+            )
+            h_codes[e], h_scales[e] = codes, scales
 
-        def second(e):
+        def second_product(e):
             if e % 2 == 0:
-                y_bank[e // 2] = [psum_y.tile([P, 2 * C], F32, name=f"y_ps{h}") for h in range(2)]
-            for h in range(2):
+                y_bank[e // 2] = [psum_y.tile([P, 2 * C], F32, name=f"y_ps{h}") for h in range(HALVES)]
+            for h in range(HALVES):
+                words = (e * N + h * P) * FP4_BYTES
                 nc.tensor.matmul_mx(
                     out=y_bank[e // 2][h][:, (e % 2) * C : (e % 2 + 1) * C],
-                    lhsT=w2_t[:, e * 2 * N + h * 2 * P : e * 2 * N + (h + 1) * 2 * P].bitcast(E2M1X4),
-                    lhsT_scale=w2_pl[:, e * N + h * P : e * N + (h + 1) * P],
+                    lhsT=w2_sb[:, words : words + FP4_BYTES * P].bitcast(E2M1X4),
+                    lhsT_scale=w2_sc[:, e * N + h * P : e * N + (h + 1) * P],
                     rhs=h_codes[e][:].bitcast(E4M3X4),
                     rhs_scale=h_scales[e][:],
                     start=True,
@@ -188,73 +226,65 @@ def tile_moe_pln_mlp_relu2_kernel(
                 )
 
         def keep_y(pair):
-            for h in range(2):
+            for h in range(HALVES):
                 dst = y_sb[h][:, 2 * C * pair : 2 * C * (pair + 1)]
                 if (pair, h) in Y_ON_VECTOR:
                     nc.vector.tensor_copy(dst, y_bank[pair][h][:])
                 else:
                     nc.scalar.copy(dst, y_bank[pair][h][:])
 
-        tokens(0)
-        gather_codes(0, 0 * C, 3 * C)
-        gather_codes(0, 3 * C, 4 * C)
-        tokens(1)
-        for e in range(E + 7):
-            if e == 0:
-                gather_scales(1, 0 * C, 1 * C)
-                gather_codes(1, 0 * C, 1 * C)
-                gather_scales(1, 1 * C, 3 * C)
-                gather_codes(1, 1 * C, 3 * C)
-                gather_scales(0, 0 * C, 3 * C)
-                gather_codes(0, 4 * C, 5 * C)
+        quantise_tokens(0)
+        for group in EARLY_GROUPS:
+            gather_codes(0, group)
+            gather_scales(0, group)
+        quantise_tokens(1)
+        g_codes[0, 1] = turns.tile([P, S - LATE * C], U32, name="g_codes0_late", tag="x_bf16_1", align_bytes=64)
+        g_scales[0, 1] = turns.tile([P, S - LATE * C], U8, name="g_scales0_late", tag="x_raw1", align_bytes=64)
+
+        def gather_both_passes(group):
+            gather_codes(0, group)
+            gather_scales(0, group)
+            gather_scales(1, group)
+            gather_codes(1, group)
+
+        for group in EARLY_GROUPS:
+            gather_scales(1, group)
+            gather_codes(1, group)
+        gather_both_passes(LATE_GROUPS[0])
+        for e in range(E + KEEP_LAG):
             if e == 1:
-                gather_scales(0, 6 * C, 8 * C)
-                gather_scales(1, 3 * C, 4 * C)
-                gather_scales(0, 3 * C, 6 * C)
-                gather_scales(1, 4 * C, 5 * C)
-            if e == 3:
-                gather_codes(1, 3 * C, 4 * C)
-                gather_codes(1, 4 * C, 5 * C)
-            if e == 4:
-                gather_codes(0, 5 * C, 6 * C)
-            if e == 5:
-                gather_codes(1, 5 * C, 8 * C)
-                gather_scales(1, 5 * C, 8 * C)
-            if e == 6:
-                gather_codes(0, 6 * C, 7 * C)
-                gather_codes(0, 7 * C, 8 * C)
+                gather_both_passes(LATE_GROUPS[1])
             if e < E:
-                first(e)
+                first_product(e)
                 relu(e)
-            if 2 <= e < E + 2:
-                turn(e - 2)
-                square(e - 2)
-            if 4 <= e < E + 4:
-                quantise_h(e - 4)
-            if 5 <= e < E + 5:
-                second(e - 5)
-            if e >= 7 and (e - 7) % 2 == 1:
-                keep_y((e - 7) // 2)
+            if TURN_LAG <= e < E + TURN_LAG:
+                turn(e - TURN_LAG)
+                square(e - TURN_LAG)
+                quantise_h(e - TURN_LAG)
+            if SECOND_LAG <= e < E + SECOND_LAG:
+                second_product(e - SECOND_LAG)
+            if e > KEEP_LAG and (e - KEEP_LAG) % 2 == 1:
+                keep_y((e - KEEP_LAG) // 2)
 
         half = T // 2
-        prods = [[keep.tile([P, T], F32, name=f"prod{h}{i}") for i in range(2)] for h in range(2)]
-        sums = [keep.tile([P, T], F32, name=f"sum{h}") for h in range(2)]
+        products = [[keep.tile([P, T], F32, name=f"product{h}{i}") for i in range(2)] for h in range(HALVES)]
+        sums = [keep.tile([P, T], F32, name=f"sum{h}") for h in range(HALVES)]
 
         def fetch(h, i, a, b):
-            pos_t = (pos1_t, pos2_t)[i]
+            pos_sb = (pos1_sb, pos2_sb)[i]
             nc.vector.tensor_tensor(
-                prods[h][i][:, a:b], y_sb[h][:].indirect(pos_t[:, a // 16 : b // 16]), gates[h][:, i, a:b], MULT
+                products[h][i][:, a:b], y_sb[h][:].indirect(pos_sb[:, a // 16 : b // 16]), gate_sb[h][:, i, a:b], MULT
             )
 
-        def add(h, a, b):
-            nc.vector.tensor_tensor(sums[h][:, a:b], prods[h][0][:, a:b], prods[h][1][:, a:b], ADD)
+        def add_and_store(h, a, b):
+            nc.vector.tensor_tensor(sums[h][:, a:b], products[h][0][:, a:b], products[h][1][:, a:b], ADD)
             nc.sync.dma_start(out=out[P * h : P * h + P, a:b], in_=sums[h][:, a:b])
 
         fetch(0, 0, 0, T)
         fetch(0, 1, 0, T)
         fetch(1, 0, 0, T)
-        add(0, 0, T)
+        add_and_store(0, 0, T)
         fetch(1, 1, 0, half)
         fetch(1, 1, half, T)
-        add(1, 0, half)
-        add(1, half, T)
+        add_and_store(1, 0, half)
+        add_and_store(1, half, T)

from contextlib import ExitStack

import concourse.mybir as mybir
from concourse.masks import make_identity

K, T, E, C, H, N = 1024, 512, 8, 128, 512, 256
S = E * C
P = 128
PACK = 4
PASS_K = P * PACK
PASSES = K // PASS_K
HALVES = N // P
FP4_BYTES = 2
PAIRS = E // 2

FLOPS = 2 * S * (K * H + H * N)

F32 = mybir.dt.float32
BF16 = mybir.dt.bfloat16
I32 = mybir.dt.int32
U32 = mybir.dt.uint32
U16 = mybir.dt.uint16
U8 = mybir.dt.uint8
E4M3X4 = mybir.dt.float8_e4m3fn_x4
E2M1X4 = mybir.dt.float4_e2m1fn_x4
MULT = mybir.AluOpType.mult
ADD = mybir.AluOpType.add
MAX = mybir.AluOpType.max
RELU = mybir.ActivationFunctionType.Relu
SQUARE = mybir.ActivationFunctionType.Square

X_ON_VECTOR = ((160, 160), (64, 128))
RELU_ON_VECTOR = (6, 7)
Y_ON_VECTOR = ((1, 1), (2, 1), (3, 1))

EARLY_GROUPS = ((0, 1), (1, 3))
LATE_GROUPS = ((3, 5), (5, 8))
LATE = LATE_GROUPS[0][0]

TURN_LAG = 2
SECOND_LAG = 5
KEEP_LAG = 7


def tile_moe_pln_mlp_relu2_kernel(
    tc, xT, w1_words, w1_scales, w2_words, w2_scales, gate, offs, pos1, pos2, out
):
    nc = tc.nc
    with ExitStack() as ctx:
        lists = ctx.enter_context(tc.tile_pool(name="lists", bufs=1))
        keep = ctx.enter_context(tc.tile_pool(name="keep", bufs=1))
        turns = ctx.enter_context(tc.tile_pool(name="turns", bufs=1))
        ring = ctx.enter_context(tc.tile_pool(name="ring", bufs=4))
        psum_a = ctx.enter_context(tc.psum_pool(name="psum_a", bufs=4))
        psum_t = ctx.enter_context(tc.psum_pool(name="psum_t", bufs=2))
        psum_y = ctx.enter_context(tc.psum_pool(name="psum_y", bufs=1))

        offs_sb = lists.tile([P, S // 16], U16, name="offs_sb")
        pos1_sb = lists.tile([P, T // 16], U16, name="pos1_sb")
        pos2_sb = lists.tile([P, T // 16], U16, name="pos2_sb")

        x_raw = [
            turns.tile([P, PACK, T], F32, name=f"x_raw{s}", tag=f"x_raw{s}", align_bytes=64) for s in range(PASSES)
        ]

        def load_x(s):
            rows = xT[PASS_K * s : PASS_K * s + PASS_K, :]
            nc.sync.dma_start(out=x_raw[s][:], in_=rows.rearrange("(p j) t -> p j t", j=PACK))

        load_x(0)
        nc.sync.dma_start(offs_sb[:], offs)
        load_x(1)

        quad = 4 * PASSES
        w1_sc = [keep.tile([P, quad * H], U8, name=f"w1_sc{k}", align_bytes=64) for k in range(2)]
        w2_sc = keep.tile([P, E * N], U8, name="w2_sc", align_bytes=64)
        nc.vector.memset(w1_sc[0][:].bitcast(I32), 0)
        nc.gpsimd.memset(w1_sc[1][:].bitcast(I32), 0)
        nc.gpsimd.memset(w2_sc[:].bitcast(I32), 0)

        def load_scales(tile, scales, count, start):
            dst = tile[:].bitcast(I32).rearrange("p (g i) -> p g i", g=count)
            src = scales.bitcast(I32).rearrange("e s q i -> q (e s) i")[:, start : start + count, :]
            for q in range(4):
                nc.sync.dma_start(out=dst[32 * q : 32 * q + 4], in_=src[4 * q : 4 * q + 4])

        pair_passes = 2 * PASSES
        w1_sb = [keep.tile([P, pair_passes * FP4_BYTES * H], U8, name=f"w1_sb{k}", align_bytes=64) for k in range(PAIRS)]
        w2_sb = keep.tile([P, E * FP4_BYTES * N], U8, name="w2_sb", align_bytes=64)

        def load_w1(pair):
            src = w1_words.bitcast(I32).rearrange("e s p c -> p (e s) c")
            nc.sync.dma_start(
                out=w1_sb[pair][:].bitcast(I32).rearrange("p (g c) -> p g c", g=pair_passes),
                in_=src[:, pair_passes * pair : pair_passes * pair + pair_passes, :],
            )

        load_w1(0)
        load_scales(w1_sc[0], w1_scales, quad, 0)
        load_w1(1)
        load_scales(w1_sc[1], w1_scales, quad, quad)
        load_w1(2)
        load_scales(w2_sc, w2_scales, E, 0)
        nc.sync.dma_start(
            out=w2_sb[:].bitcast(I32).rearrange("p (g c) -> p g c", g=E),
            in_=w2_words.bitcast(I32).rearrange("e s p c -> p (e s) c"),
        )
        load_w1(3)
        nc.sync.dma_start(pos1_sb[:], pos1)
        nc.sync.dma_start(pos2_sb[:], pos2)
        gate_sb = []
        for h in range(HALVES):
            gate_half = keep.tile([P, 2, T], F32, name=f"gate_half{h}")
            nc.sync.dma_start(out=gate_half[:], in_=gate[:, P * h : P * h + P, :].rearrange("g n t -> n g t"))
            gate_sb.append(gate_half)

        warm = keep.tile([P, 1], F32, name="warm")
        nc.gpsimd.memset(warm[:], 0.0)
        nc.scalar.activation(warm[:], warm[:], SQUARE)
        x_scales = [keep.tile([P, T], U8, name=f"x_scales{s}", align_bytes=64) for s in range(PASSES)]
        for s in range(PASSES):
            nc.gpsimd.memset(x_scales[s][:], 0)
        ident = keep.tile([P, P], F32, name="ident")
        make_identity(nc, ident[:])

        x_codes = [keep.tile([P, T], U32, name=f"x_codes{s}", align_bytes=64) for s in range(PASSES)]
        g_codes = {
            (0, 0): keep.tile([P, LATE * C], U32, name="g_codes0_early", align_bytes=64),
            (1, 0): keep.tile([P, S], U32, name="g_codes1", align_bytes=64),
        }
        g_scales = {
            (0, 0): keep.tile([P, LATE * C], U8, name="g_scales0_early", align_bytes=64),
            (1, 0): keep.tile([P, S], U8, name="g_scales1", align_bytes=64),
        }

        def slots(tiles, s, a, b):
            late = s == 0 and a >= LATE * C
            start = LATE * C if late else 0
            return tiles[s, int(late)][:, a - start : b - start]

        def quantise_tokens(s):
            x_bf16 = turns.tile([P, T, PACK], BF16, name=f"x_bf16_{s}", tag=f"x_bf16_{s}", align_bytes=64)
            half = T // 2
            src = x_raw[s][:].rearrange("p j (c i) -> p c j i", i=4)
            dst = x_bf16[:].rearrange("p (c i) j -> p c j i", i=4)
            for part in range(2):
                a, b = half * part, half * part + half
                m = a + X_ON_VECTOR[s][part]
                nc.vector.tensor_copy(dst[:, a // 4 : m // 4], src[:, a // 4 : m // 4])
                nc.scalar.copy(dst[:, m // 4 : b // 4], src[:, m // 4 : b // 4])
                nc.vector.quantize_mx(
                    out=x_codes[s][:, a:b].bitcast(E4M3X4),
                    scales=x_scales[s][:, a:b],
                    in_=x_bf16[:, a:b, :].rearrange("p t j -> p (t j)"),
                )

        def gather_codes(s, group):
            a, b = group[0] * C, group[1] * C
            nc.vector.tensor_copy(slots(g_codes, s, a, b), x_codes[s][:].indirect(offs_sb[:, a // 16 : b // 16]))

        def gather_scales(s, group):
            a, b = group[0] * C, group[1] * C
            nc.vector.tensor_copy(slots(g_scales, s, a, b), x_scales[s][:].indirect(offs_sb[:, a // 16 : b // 16]))

        a_bank, relu_sb, turned, h_bf16, h_codes, h_scales, y_bank = {}, {}, {}, {}, {}, {}, {}
        y_sb = [keep.tile([P, S], F32, name=f"y_sb{h}") for h in range(HALVES)]

        def first_product(e):
            a_ps = psum_a.tile([P, H], F32, name="a_ps")
            for s in range(PASSES):
                in_pair = (e % 2) * PASSES + s
                in_quad = (e % 4) * PASSES + s
                nc.tensor.matmul_mx(
                    out=a_ps[:],
                    lhsT=slots(g_codes, s, C * e, C * e + C).bitcast(E4M3X4),
                    lhsT_scale=slots(g_scales, s, C * e, C * e + C),
                    rhs=w1_sb[e // 2][:, in_pair * FP4_BYTES * H : (in_pair + 1) * FP4_BYTES * H].bitcast(E2M1X4),
                    rhs_scale=w1_sc[e // 4][:, in_quad * H : (in_quad + 1) * H],
                    start=(s == 0),
                    stop=(s == PASSES - 1),
                )
            a_bank[e] = a_ps

        def relu(e):
            r = ring.tile([P, PACK, P], F32, name="r")
            src = a_bank[e][:].rearrange("p (m t) -> p m t", t=PACK)
            dst = r[:].rearrange("p t m -> p m t")
            if e in RELU_ON_VECTOR:
                nc.vector.tensor_scalar(dst, src, 0.0, None, MAX)
            else:
                nc.scalar.activation(dst, src, RELU)
            relu_sb[e] = r

        def turn(e):
            t_ps = psum_t.tile([P, PACK, P], F32, name="t_ps")
            for t in range(PACK):
                nc.tensor.transpose(t_ps[:, t, :], relu_sb[e][:, t, :], ident[:])
            turned[e] = t_ps

        def square(e):
            h_sb = ring.tile([P, P, PACK], BF16, name="h_sb", align_bytes=64)
            nc.scalar.activation(h_sb[:], turned[e][:].rearrange("p t c -> p c t"), SQUARE)
            h_bf16[e] = h_sb

        def quantise_h(e):
            codes = ring.tile([P, P], U32, name="codes", align_bytes=64)
            scales = ring.tile([P, P], U8, name="scales", align_bytes=64)
            nc.vector.quantize_mx(
                out=codes[:].bitcast(E4M3X4), scales=scales[:], in_=h_bf16[e][:].rearrange("p c t -> p (c t)")
            )
            h_codes[e], h_scales[e] = codes, scales

        def second_product(e):
            if e % 2 == 0:
                y_bank[e // 2] = [psum_y.tile([P, 2 * C], F32, name=f"y_ps{h}") for h in range(HALVES)]
            for h in range(HALVES):
                words = (e * N + h * P) * FP4_BYTES
                nc.tensor.matmul_mx(
                    out=y_bank[e // 2][h][:, (e % 2) * C : (e % 2 + 1) * C],
                    lhsT=w2_sb[:, words : words + FP4_BYTES * P].bitcast(E2M1X4),
                    lhsT_scale=w2_sc[:, e * N + h * P : e * N + (h + 1) * P],
                    rhs=h_codes[e][:].bitcast(E4M3X4),
                    rhs_scale=h_scales[e][:],
                    start=True,
                    stop=True,
                )

        def keep_y(pair):
            for h in range(HALVES):
                dst = y_sb[h][:, 2 * C * pair : 2 * C * (pair + 1)]
                if (pair, h) in Y_ON_VECTOR:
                    nc.vector.tensor_copy(dst, y_bank[pair][h][:])
                else:
                    nc.scalar.copy(dst, y_bank[pair][h][:])

        quantise_tokens(0)
        for group in EARLY_GROUPS:
            gather_codes(0, group)
            gather_scales(0, group)
        quantise_tokens(1)
        g_codes[0, 1] = turns.tile([P, S - LATE * C], U32, name="g_codes0_late", tag="x_bf16_1", align_bytes=64)
        g_scales[0, 1] = turns.tile([P, S - LATE * C], U8, name="g_scales0_late", tag="x_raw1", align_bytes=64)

        def gather_both_passes(group):
            gather_codes(0, group)
            gather_scales(0, group)
            gather_scales(1, group)
            gather_codes(1, group)

        for group in EARLY_GROUPS:
            gather_scales(1, group)
            gather_codes(1, group)
        gather_both_passes(LATE_GROUPS[0])
        for e in range(E + KEEP_LAG):
            if e == 1:
                gather_both_passes(LATE_GROUPS[1])
            if e < E:
                first_product(e)
                relu(e)
            if TURN_LAG <= e < E + TURN_LAG:
                turn(e - TURN_LAG)
                square(e - TURN_LAG)
                quantise_h(e - TURN_LAG)
            if SECOND_LAG <= e < E + SECOND_LAG:
                second_product(e - SECOND_LAG)
            if e > KEEP_LAG and (e - KEEP_LAG) % 2 == 1:
                keep_y((e - KEEP_LAG) // 2)

        half = T // 2
        products = [[keep.tile([P, T], F32, name=f"product{h}{i}") for i in range(2)] for h in range(HALVES)]
        sums = [keep.tile([P, T], F32, name=f"sum{h}") for h in range(HALVES)]

        def fetch(h, i, a, b):
            pos_sb = (pos1_sb, pos2_sb)[i]
            nc.vector.tensor_tensor(
                products[h][i][:, a:b], y_sb[h][:].indirect(pos_sb[:, a // 16 : b // 16]), gate_sb[h][:, i, a:b], MULT
            )

        def add_and_store(h, a, b):
            nc.vector.tensor_tensor(sums[h][:, a:b], products[h][0][:, a:b], products[h][1][:, a:b], ADD)
            nc.sync.dma_start(out=out[P * h : P * h + P, a:b], in_=sums[h][:, a:b])

        fetch(0, 0, 0, T)
        fetch(0, 1, 0, T)
        fetch(1, 0, 0, T)
        add_and_store(0, 0, T)
        fetch(1, 1, 0, half)
        fetch(1, 1, half, T)
        add_and_store(1, 0, half)
        add_and_store(1, half, T)
